import numpy as np
import ml_dtypes


def mxq(x, axis, fmt="e4m3"):
    dtype, down = {"e4m3": (ml_dtypes.float8_e4m3fn, 7), "e5m2": (ml_dtypes.float8_e5m2, 14)}[fmt]
    v = np.moveaxis(np.asarray(x, np.float32).astype(ml_dtypes.bfloat16).astype(np.float64), axis, -1)
    blocks = v.reshape(v.shape[:-1] + (-1, 32))
    amax = np.abs(blocks).max(-1, keepdims=True)
    byte = np.maximum(np.where(amax > 0, np.frexp(amax)[1] - 1 + 127, 0) - down, 1)
    scale = np.exp2(byte - 127.0)
    codes = (blocks / scale).astype(np.float32).astype(dtype).astype(np.float64)
    return np.moveaxis((codes * scale).reshape(v.shape), -1, axis)


WIDE = False


def mx_kscale(k):
    if not WIDE:
        return np.ones(k)
    levels = np.array([24, -24, 12, -12, 0])
    if k % 512:
        return np.exp2(np.random.permutation(np.resize(levels, k // 32))).repeat(32)
    a = np.empty((k // 512, 16))
    for p in range(k // 512):
        a[p, :8] = np.random.permutation(np.resize(levels, 8))
        for g in range(8):
            far = levels[np.abs(levels - a[p, g]) >= 10]
            a[p, g + 8] = far[np.random.randint(len(far))]
    return np.exp2(a.ravel()).repeat(32)


def f64(x):
    return np.asarray(x).astype(np.float64)


def striped(idx):
    return np.tile(idx.reshape(-1, 16).T, (8, 1)).astype(np.uint16)


def unstriped(offs):
    return offs[:16].T.reshape(-1).astype(np.int64)


E2M1 = np.array([0.0, 0.5, 1.0, 1.5, 2.0, 3.0, 4.0, 6.0, -0.0, -0.5, -1.0, -1.5, -2.0, -3.0, -4.0, -6.0])


def pack_weight(w, fmt):
    k, n = w.shape
    w = f64(np.asarray(w, np.float32).astype(ml_dtypes.bfloat16)).reshape(k // 32, 32, n)
    amax = np.abs(w).max(1)
    if fmt == "e4m3":
        byte = np.frexp(amax)[1] - 1 + 127 - 7
    else:
        mant, ex = np.frexp(amax / 6.0)
        byte = np.where(mant > 0.5, ex, ex - 1) + 127
    byte = np.clip(np.where(amax > 0, byte, 1), 1, 254)
    scaled = (w * np.exp2(127.0 - byte)[:, None, :]).reshape(k, n).astype(np.float32)
    by_word = np.ascontiguousarray(scaled.reshape(k // 512, 128, 4, n).transpose(0, 1, 3, 2))
    if fmt == "e4m3":
        words = by_word.astype(ml_dtypes.float8_e4m3fn).view(np.uint8)
    else:
        c = by_word.astype(ml_dtypes.float4_e2m1fn).view(np.uint8) & 0xF
        words = (c[..., 0::2] | (c[..., 1::2] << 4)).reshape(k // 512, 128, 2 * n)
    return np.ascontiguousarray(words), np.ascontiguousarray(byte.astype(np.uint8).reshape(k // 512, 16, n))


def unpack_weight(words, scales, fmt):
    g, _, n = scales.shape
    words = np.ascontiguousarray(words).reshape(g, 128, n, -1)
    if fmt == "e4m3":
        vals = words.view(ml_dtypes.float8_e4m3fn).astype(np.float64)
    else:
        nib = np.empty((g, 128, n, 4), np.uint8)
        nib[..., 0::2] = words & 0xF
        nib[..., 1::2] = words >> 4
        vals = E2M1[nib]
    vals = vals * np.repeat(np.exp2(scales.astype(np.float64) - 127.0), 8, axis=1)[..., None]
    return vals.transpose(0, 1, 3, 2).reshape(g * 512, n)


K, F, N, T, J = 512, 1024, 128, 4096, 1024


def setup_inputs():
    n = np.random.standard_normal
    s = mx_kscale(K)[:, None]
    u = mx_kscale(F)[:, None]
    p_tab = pack_weight(n((K, T)) * s, "e4m3")
    p_co = pack_weight(n((K, F)) / np.sqrt(K) / s, "e2m1")
    p_si = pack_weight(n((K, F)) / np.sqrt(K) / s, "e2m1")
    p_fb = pack_weight(np.abs(n((F, N))) / F / u, "e4m3")
    return {
        "tab_words": p_tab[0],
        "tab_scales": p_tab[1],
        "co_words": p_co[0],
        "co_scales": p_co[1],
        "si_words": p_si[0],
        "si_scales": p_si[1],
        "gn": (np.random.uniform(0.5, 2.0, F) * u[:, 0]).astype(np.float32),
        "fb_words": p_fb[0],
        "fb_scales": p_fb[1],
        "mu": (np.random.uniform(0.5, 1.5, N)).astype(np.float32),
        "isd": (np.random.uniform(0.5, 2.0, N)).astype(np.float32),
        "offs": striped(np.random.permutation(T)[:J]),
    }


def reference(tab_words, tab_scales, co_words, co_scales, si_words, si_scales, gn, fb_words, fb_scales, mu, isd, offs):
    idx = unstriped(offs)
    tab_ = unpack_weight(tab_words, tab_scales, "e4m3")[:, idx]
    co_ = unpack_weight(co_words, co_scales, "e2m1")
    si_ = unpack_weight(si_words, si_scales, "e2m1")
    re = co_.T @ tab_
    im = si_.T @ tab_
    h = f64(gn)[:, None] * ((re) ** 2 + (im) ** 2)
    h_ = mxq(h, 0, "e4m3")
    fb_ = unpack_weight(fb_words, fb_scales, "e4m3")
    y = fb_.T @ h_
    return (y - f64(mu)[:, None]) * f64(isd)[:, None]

@@ -1,0 +1,192 @@
+from contextlib import ExitStack
+
+import concourse.mybir as mybir
+
+K, F, N, T, J = 512, 1024, 128, 4096, 1024
+FLOPS = 2 * (2 * K * F * J + F * N * J)
+
+F32 = mybir.dt.float32
+BF16 = mybir.dt.bfloat16
+I32 = mybir.dt.int32
+U32 = mybir.dt.uint32
+U16 = mybir.dt.uint16
+U8 = mybir.dt.uint8
+FP8X4 = mybir.dt.float8_e4m3fn_x4
+FP4X4 = mybir.dt.float4_e2m1fn_x4
+ALU = mybir.AluOpType
+ACT = mybir.ActivationFunctionType
+
+P = 128
+PACK = 4
+PASSES = F // (P * PACK)
+HALF = 512
+WIDTHS = (256, 256, 256, 128, 128)
+WMAX = max(WIDTHS)
+ROW_STEP = 8
+FILL = 64
+
+
+def tile_list_meltab_norm_kernel(
+    tc, tab_words, tab_scales, co_words, co_scales, si_words, si_scales, gn, fb_words, fb_scales, mu, isd, offs, out
+):
+    nc = tc.nc
+    with ExitStack() as ctx:
+        keep = ctx.enter_context(tc.tile_pool(name="keep", bufs=1))
+        work = ctx.enter_context(tc.tile_pool(name="work", bufs=3))
+        zpool = ctx.enter_context(tc.psum_pool(name="zpool", bufs=6))
+        ypool = ctx.enter_context(tc.psum_pool(name="ypool", bufs=2))
+
+        offsets = keep.tile([P, J // 16], U16, name="offsets")
+        tab_s = keep.tile([P, T], U8, name="tab_s", align_bytes=64)
+        raw_s = keep.tile([P, 2 * F], U8, name="raw_s", align_bytes=64)
+        early = keep.tile([P, HALF + 2 * F], U8, name="early", align_bytes=64)
+        late = keep.tile([P, HALF + PASSES * N], U8, name="late", align_bytes=64)
+        raw_w = [keep.tile([P, 2 * F], U8, name="raw_w%d" % i, align_bytes=64) for i in range(2)]
+        wts = [keep.tile([P, 2 * F], U8, name="wts%d" % i, align_bytes=64) for i in range(2)]
+        fb_w = keep.tile([P, PASSES, N], U32, name="fb_w", align_bytes=64)
+        gain = keep.tile([P, PASSES * PACK], F32, name="gain")
+        mu_c = keep.tile([P, 1], F32, name="mu_c")
+        isd_c = keep.tile([P, 1], F32, name="isd_c")
+
+        nc.vector.memset(tab_s[:].bitcast(I32), 0)
+        nc.vector.memset(raw_s[:].bitcast(I32), 0)
+        tab_w = keep.tile([P, T], U32, name="tab_w", tag="table", align_bytes=64)
+
+        nc.scalar.dma_start(out=tab_s[0:P:ROW_STEP, :].bitcast(I32), in_=tab_scales[0].bitcast(I32))
+        nc.scalar.dma_start(out=raw_s[0:P:ROW_STEP, 0:F].bitcast(I32), in_=co_scales[0].bitcast(I32))
+        nc.scalar.dma_start(out=raw_s[0:P:ROW_STEP, F:].bitcast(I32), in_=si_scales[0].bitcast(I32))
+        nc.sync.dma_start(offsets[:], offs)
+        nc.sync.dma_start(out=raw_w[0][:].bitcast(I32), in_=co_words[0].bitcast(I32))
+        nc.sync.dma_start(out=raw_w[1][:].bitcast(I32), in_=si_words[0].bitcast(I32))
+        nc.sync.dma_start(out=tab_w[:].bitcast(I32), in_=tab_words[0].rearrange("p t i -> p (t i)").bitcast(I32))
+        nc.sync.dma_start(out=fb_w[:].bitcast(I32), in_=fb_words.rearrange("a p n i -> p a (n i)").bitcast(I32))
+
+        nc.gpsimd.dma_start(
+            out=gain[:].rearrange("p (b t) -> p b t", t=PACK), in_=gn.rearrange("(b p t) -> p b t", p=P, t=PACK)
+        )
+        nc.gpsimd.memset(late[:, HALF:].bitcast(I32), 0)
+        nc.gpsimd.dma_start(
+            out=late[0:P:ROW_STEP, HALF:].bitcast(I32).rearrange("q (a n) -> q a n", a=PASSES),
+            in_=fb_scales.bitcast(I32).rearrange("a q n -> q a n"),
+        )
+        mag = keep.tile([P, PASSES * PACK], F32, name="mag")
+        sgn = keep.tile([P, PASSES * PACK], BF16, name="sgn")
+        half = keep.tile([P, PASSES * PACK], F32, name="half")
+        root = keep.tile([P, PASSES * PACK], F32, name="root")
+        nc.scalar.activation(out=mag[:], in_=gain[:], func=ACT.Abs)
+        nc.scalar.activation(out=sgn[:], in_=gain[:], func=ACT.Sign)
+        nc.gpsimd.memset(half[:], 0.5)
+        nc.gpsimd.tensor_tensor(root[:], mag[:], half[:], ALU.pow)
+        with nc.allow_non_contiguous_dma(reason="one value a partition"):
+            nc.gpsimd.dma_start(out=mu_c[:], in_=mu.rearrange("(p o) -> p o", o=1))
+            nc.gpsimd.dma_start(out=isd_c[:], in_=isd.rearrange("(p o) -> p o", o=1))
+
+        for i in range(2):
+            nc.vector.tensor_copy(
+                wts[i][:].bitcast(U16).rearrange("p (b t m) -> p b t m", t=PACK, m=P),
+                raw_w[i][:].bitcast(U16).rearrange("p (b m t) -> p b t m", t=PACK, m=P),
+            )
+        lists = [offsets[:, g * (HALF // 16) : (g + 1) * (HALF // 16)] for g in range(2)]
+        planes = (early, late)
+        for g in range(2):
+            got_s = keep.tile([P, HALF], U8, name="got_s%d" % g, tag="got%d" % g, align_bytes=64)
+            nc.vector.tensor_copy(got_s[:], tab_s[:].indirect(lists[g]))
+            if g == 0:
+                nc.vector.tensor_copy(
+                    early[:, HALF:].rearrange("p (b t m) -> p b t m", t=PACK, m=P),
+                    raw_s[:].rearrange("p (b m t) -> p b t m", t=PACK, m=P),
+                )
+            nc.vector.tensor_copy(planes[g][:, 0:HALF].bitcast(I32), got_s[:].bitcast(I32))
+            for r in range(1, 4):
+                nc.scalar.dma_start(
+                    out=planes[g][r:P:32, :].bitcast(I32), in_=planes[g][ROW_STEP * r : P : 32, :].bitcast(I32)
+                )
+        got_w = []
+        for g in range(2):
+            picked = keep.tile([P, HALF], U32, name="got_w%d" % g, tag="got%d" % (1 - g), align_bytes=64)
+            nc.vector.tensor_copy(picked[:], tab_w[:].indirect(lists[g]))
+            got_w.append(picked)
+
+        units = [(sum(WIDTHS[:c]), w, b) for c, w in enumerate(WIDTHS) for b in range(PASSES)]
+        squares, power, signed, acc = {}, {}, {}, {}
+
+        def transform(u):
+            j0, w, b = units[u]
+            g, c0 = divmod(j0, HALF)
+            sq = work.tile([P, PACK, 2 * w], F32, name="sq")
+            for t in range(PACK):
+                s = b * PACK + t
+                z = zpool.tile([P, 2 * w], F32, name="z")
+                for i in range(2):
+                    base = HALF + F * i + P * s
+                    nc.tensor.matmul_mx(
+                        out=z[:, i * w : (i + 1) * w],
+                        lhsT=wts[i][:, 2 * P * s : 2 * P * (s + 1)].bitcast(FP4X4),
+                        lhsT_scale=early[:, base : base + P],
+                        rhs=got_w[g][:, c0 : c0 + w].bitcast(FP8X4),
+                        rhs_scale=planes[g][:, c0 : c0 + w],
+                        start=True,
+                        stop=True,
+                    )
+                nc.scalar.activation(out=sq[:, t, :], in_=z[:], func=ACT.Square, scale=root[:, s : s + 1])
+            squares[u] = sq
+
+        def add(u):
+            w = units[u][1]
+            sq = squares[u]
+            h = work.tile([P, w * PACK], BF16, name="h", align_bytes=64)
+            nc.vector.tensor_tensor(
+                h[:].rearrange("p (c i t) -> p c t i", i=2, t=PACK),
+                sq[:, :, 0:w].rearrange("p t (c i) -> p c t i", i=2),
+                sq[:, :, w:].rearrange("p t (c i) -> p c t i", i=2),
+                ALU.add,
+            )
+            power[u] = h
+
+        def sign(u):
+            j0, w, b = units[u]
+            hs = work.tile([P, w * PACK], BF16, name="hs", align_bytes=64)
+            nc.vector.tensor_tensor(
+                hs[:].rearrange("p (c t) -> p c t", t=PACK),
+                power[u][:].rearrange("p (c t) -> p c t", t=PACK),
+                sgn[:, b * PACK : (b + 1) * PACK].unsqueeze(1).to_broadcast([P, w, PACK]),
+                ALU.mult,
+            )
+            signed[u] = hs
+
+        def filters(u):
+            j0, w, b = units[u]
+            codes = work.tile([P, w], U32, name="codes", align_bytes=64)
+            scales = work.tile([P, w], U8, name="scales", align_bytes=64)
+            nc.vector.quantize_mx(out=codes[:].bitcast(FP8X4), scales=scales[:], in_=signed[u][:])
+            if b == 0:
+                acc[j0] = ypool.tile([P, w], F32, name="y")
+            nc.tensor.matmul_mx(
+                out=acc[j0][:],
+                lhsT=fb_w[:, b, :].bitcast(FP8X4),
+                lhsT_scale=late[:, HALF + N * b : HALF + N * (b + 1)],
+                rhs=codes[:].bitcast(FP8X4),
+                rhs_scale=scales[:],
+                start=(b == 0),
+                stop=(b == PASSES - 1),
+            )
+
+        def finish(u):
+            j0, w, b = units[u]
+            if b == PASSES - 1:
+                res = work.tile([P, w], F32, name="res")
+                nc.vector.tensor_scalar(res[:], acc[j0][:], mu_c[:], isd_c[:], ALU.subtract, ALU.mult)
+                nc.sync.dma_start(out=out[:, j0 : j0 + w], in_=res[:])
+
+        n = len(units)
+        for step in range(n + 3):
+            if step < n:
+                transform(step)
+            if 0 <= step - 1 < n:
+                add(step - 1)
+            if 0 <= step - 2 < n:
+                filters(step - 2)
+            if 0 <= step - 1 < n:
+                sign(step - 1)
+            if 0 <= step - 3 < n:
+                finish(step - 3)

@@ -21,9 +21,10 @@ PACK = 4
 PASSES = F // (P * PACK)
 HALF = 512
 WIDTHS = (256, 256, 256, 128, 128)
-WMAX = max(WIDTHS)
 ROW_STEP = 8
 FILL = 64
+TINY = 2.0**-112
+TAIL = 512
 
 
 def tile_list_meltab_norm_kernel(
@@ -37,49 +38,59 @@ def tile_list_meltab_norm_kernel(
         ypool = ctx.enter_context(tc.psum_pool(name="ypool", bufs=2))
 
         offsets = keep.tile([P, J // 16], U16, name="offsets")
-        tab_s = keep.tile([P, T], U8, name="tab_s", align_bytes=64)
-        raw_s = keep.tile([P, 2 * F], U8, name="raw_s", align_bytes=64)
+        tab_s = keep.tile([P, T], U8, name="tab_s", tag="tab_s", align_bytes=64)
+        raw_s = [
+            keep.tile([P, F], U8, name="raw_s0", align_bytes=64),
+            keep.tile([P, F], U8, name="raw_s1", align_bytes=64),
+        ]
         early = keep.tile([P, HALF + 2 * F], U8, name="early", align_bytes=64)
         late = keep.tile([P, HALF + PASSES * N], U8, name="late", align_bytes=64)
-        raw_w = [keep.tile([P, 2 * F], U8, name="raw_w%d" % i, align_bytes=64) for i in range(2)]
+        raw_w = [keep.tile([P, 2 * F], U8, name="raw_w%d" % i, tag="raw_w%d" % i, align_bytes=64) for i in range(2)]
         wts = [keep.tile([P, 2 * F], U8, name="wts%d" % i, align_bytes=64) for i in range(2)]
-        fb_w = keep.tile([P, PASSES, N], U32, name="fb_w", align_bytes=64)
-        gain = keep.tile([P, PASSES * PACK], F32, name="gain")
-        mu_c = keep.tile([P, 1], F32, name="mu_c")
-        isd_c = keep.tile([P, 1], F32, name="isd_c")
+        gain = keep.tile([P, PASSES * PACK], F32, name="gain", tag="gain")
 
-        nc.vector.memset(tab_s[:].bitcast(I32), 0)
-        nc.vector.memset(raw_s[:].bitcast(I32), 0)
+        zeros = keep.tile([P, FILL], I32, name="zeros", tag="table", align_bytes=64)
+        nc.gpsimd.memset(tab_s[:].bitcast(I32), 0)
+        nc.vector.memset(zeros[:], 0)
+        for i in range(2):
+            nc.vector.tensor_copy(
+                raw_s[i][:].bitcast(I32).rearrange("p (a c) -> p a c", c=FILL),
+                zeros[:].unsqueeze(1).to_broadcast([P, F // 4 // FILL, FILL]),
+            )
+        stage = [
+            keep.tile([P, HALF + 2 * F], U8, name="stage0", tag="stage0", align_bytes=64),
+            keep.tile([P, HALF + PASSES * N], U8, name="stage1", tag="stage1", align_bytes=64),
+        ]
+        nc.gpsimd.memset(early[:].bitcast(I32), 0)
+        nc.gpsimd.memset(late[:].bitcast(I32), 0)
+        nc.gpsimd.memset(stage[1][:, HALF:].bitcast(I32), 0)
         tab_w = keep.tile([P, T], U32, name="tab_w", tag="table", align_bytes=64)
 
-        nc.scalar.dma_start(out=tab_s[0:P:ROW_STEP, :].bitcast(I32), in_=tab_scales[0].bitcast(I32))
-        nc.scalar.dma_start(out=raw_s[0:P:ROW_STEP, 0:F].bitcast(I32), in_=co_scales[0].bitcast(I32))
-        nc.scalar.dma_start(out=raw_s[0:P:ROW_STEP, F:].bitcast(I32), in_=si_scales[0].bitcast(I32))
         nc.sync.dma_start(offsets[:], offs)
         nc.sync.dma_start(out=raw_w[0][:].bitcast(I32), in_=co_words[0].bitcast(I32))
         nc.sync.dma_start(out=raw_w[1][:].bitcast(I32), in_=si_words[0].bitcast(I32))
-        nc.sync.dma_start(out=tab_w[:].bitcast(I32), in_=tab_words[0].rearrange("p t i -> p (t i)").bitcast(I32))
-        nc.sync.dma_start(out=fb_w[:].bitcast(I32), in_=fb_words.rearrange("a p n i -> p a (n i)").bitcast(I32))
-
-        nc.gpsimd.dma_start(
+        nc.scalar.dma_start(
             out=gain[:].rearrange("p (b t) -> p b t", t=PACK), in_=gn.rearrange("(b p t) -> p b t", p=P, t=PACK)
         )
-        nc.gpsimd.memset(late[:, HALF:].bitcast(I32), 0)
-        nc.gpsimd.dma_start(
-            out=late[0:P:ROW_STEP, HALF:].bitcast(I32).rearrange("q (a n) -> q a n", a=PASSES),
+        nc.sync.dma_start(out=tab_s[0:P:ROW_STEP, :].bitcast(I32), in_=tab_scales[0].bitcast(I32))
+        nc.sync.dma_start(out=raw_s[0][0:P:ROW_STEP, :].bitcast(I32), in_=co_scales[0].bitcast(I32))
+        nc.sync.dma_start(out=raw_s[1][0:P:ROW_STEP, :].bitcast(I32), in_=si_scales[0].bitcast(I32))
+        nc.sync.dma_start(out=tab_w[:].bitcast(I32), in_=tab_words[0].rearrange("p t i -> p (t i)").bitcast(I32))
+        nc.sync.dma_start(
+            out=stage[1][0:P:ROW_STEP, HALF:].bitcast(I32).rearrange("q (a n) -> q a n", a=PASSES),
             in_=fb_scales.bitcast(I32).rearrange("a q n -> q a n"),
         )
-        mag = keep.tile([P, PASSES * PACK], F32, name="mag")
-        sgn = keep.tile([P, PASSES * PACK], BF16, name="sgn")
-        half = keep.tile([P, PASSES * PACK], F32, name="half")
-        root = keep.tile([P, PASSES * PACK], F32, name="root")
+
+        small = [P, PASSES * PACK]
+        mag = keep.tile(small, F32, name="mag")
+        sgn = keep.tile(small, BF16, name="sgn")
+        guess = keep.tile(small, F32, name="guess")
+        inv = keep.tile(small, F32, name="inv")
+        quot = keep.tile(small, F32, name="quot")
+        root = keep.tile(small, F32, name="root")
         nc.scalar.activation(out=mag[:], in_=gain[:], func=ACT.Abs)
+        nc.scalar.activation(out=guess[:], in_=mag[:], func=ACT.Sqrt, bias=TINY)
         nc.scalar.activation(out=sgn[:], in_=gain[:], func=ACT.Sign)
-        nc.gpsimd.memset(half[:], 0.5)
-        nc.gpsimd.tensor_tensor(root[:], mag[:], half[:], ALU.pow)
-        with nc.allow_non_contiguous_dma(reason="one value a partition"):
-            nc.gpsimd.dma_start(out=mu_c[:], in_=mu.rearrange("(p o) -> p o", o=1))
-            nc.gpsimd.dma_start(out=isd_c[:], in_=isd.rearrange("(p o) -> p o", o=1))
 
         for i in range(2):
             nc.vector.tensor_copy(
@@ -88,24 +99,47 @@ def tile_list_meltab_norm_kernel(
             )
         lists = [offsets[:, g * (HALF // 16) : (g + 1) * (HALF // 16)] for g in range(2)]
         planes = (early, late)
-        for g in range(2):
-            got_s = keep.tile([P, HALF], U8, name="got_s%d" % g, tag="got%d" % g, align_bytes=64)
+
+        def look_up_scales(g):
+            got_s = keep.tile([P, HALF], U8, name="got_s%d" % g, tag=("got0", "stage0")[g], align_bytes=64)
             nc.vector.tensor_copy(got_s[:], tab_s[:].indirect(lists[g]))
-            if g == 0:
-                nc.vector.tensor_copy(
-                    early[:, HALF:].rearrange("p (b t m) -> p b t m", t=PACK, m=P),
-                    raw_s[:].rearrange("p (b m t) -> p b t m", t=PACK, m=P),
+            nc.vector.tensor_copy(stage[g][:, 0:HALF].bitcast(I32), got_s[:].bitcast(I32))
+
+        def place_rows(g):
+            for r in range(4):
+                (nc.scalar if g == 0 and r % 2 == 0 else nc.sync).dma_start(
+                    out=planes[g][r:P:32, :].bitcast(I32), in_=stage[g][ROW_STEP * r : P : 32, :].bitcast(I32)
                 )
-            nc.vector.tensor_copy(planes[g][:, 0:HALF].bitcast(I32), got_s[:].bitcast(I32))
-            for r in range(1, 4):
-                nc.scalar.dma_start(
-                    out=planes[g][r:P:32, :].bitcast(I32), in_=planes[g][ROW_STEP * r : P : 32, :].bitcast(I32)
-                )
-        got_w = []
-        for g in range(2):
-            picked = keep.tile([P, HALF], U32, name="got_w%d" % g, tag="got%d" % (1 - g), align_bytes=64)
+
+        def look_up_words(g):
+            picked = keep.tile([P, HALF], U32, name="got_w%d" % g, tag=("got0", "stage0")[g], align_bytes=64)
             nc.vector.tensor_copy(picked[:], tab_w[:].indirect(lists[g]))
-            got_w.append(picked)
+            return picked
+
+        look_up_scales(0)
+        for i in range(2):
+            nc.vector.tensor_copy(
+                stage[0][:, HALF + F * i : HALF + F * (i + 1)].rearrange("p (b t m) -> p b t m", t=PACK, m=P),
+                raw_s[i][:].rearrange("p (b m t) -> p b t m", t=PACK, m=P),
+            )
+        place_rows(0)
+        fb_w = keep.tile([P, PASSES, N], U32, name="fb_w", tag="raw_w0", align_bytes=64)
+        nc.sync.dma_start(out=fb_w[:].bitcast(I32), in_=fb_words.rearrange("a p n i -> p a (n i)").bitcast(I32))
+        nc.vector.reciprocal(inv[:], guess[:])
+        nc.vector.scalar_tensor_tensor(quot[:], mag[:], 0.5, inv[:], ALU.mult, ALU.mult)
+        nc.vector.scalar_tensor_tensor(root[:], guess[:], 0.5, quot[:], ALU.mult, ALU.add)
+        got_w = [look_up_words(0)]
+        look_up_scales(1)
+        place_rows(1)
+        got_w.append(look_up_words(1))
+
+        mu_c = keep.tile([P, 1], F32, name="mu_c", tag="gain")
+        isd_c = keep.tile([P, 1], F32, name="isd_c", tag="tab_s", align_bytes=64)
+        shift = keep.tile([P, 1], F32, name="shift")
+        with nc.allow_non_contiguous_dma(reason="one value a partition"):
+            nc.sync.dma_start(out=mu_c[:], in_=mu.rearrange("(p o) -> p o", o=1))
+            nc.sync.dma_start(out=isd_c[:], in_=isd.rearrange("(p o) -> p o", o=1))
+        nc.gpsimd.tensor_scalar(shift[:], mu_c[:], isd_c[:], -1.0, ALU.mult, ALU.mult)
 
         units = [(sum(WIDTHS[:c]), w, b) for c, w in enumerate(WIDTHS) for b in range(PASSES)]
         squares, power, signed, acc = {}, {}, {}, {}
@@ -175,7 +209,10 @@ def tile_list_meltab_norm_kernel(
             j0, w, b = units[u]
             if b == PASSES - 1:
                 res = work.tile([P, w], F32, name="res")
-                nc.vector.tensor_scalar(res[:], acc[j0][:], mu_c[:], isd_c[:], ALU.subtract, ALU.mult)
+                if j0 + w > J - TAIL:
+                    nc.scalar.activation(out=res[:], in_=acc[j0][:], func=ACT.Identity, scale=isd_c[:], bias=shift[:])
+                else:
+                    nc.vector.tensor_scalar(res[:], acc[j0][:], isd_c[:], shift[:], ALU.mult, ALU.add)
                 nc.sync.dma_start(out=out[:, j0 : j0 + w], in_=res[:])
 
         n = len(units)

@@ -34,8 +34,8 @@ def tile_list_meltab_norm_kernel(
     with ExitStack() as ctx:
         keep = ctx.enter_context(tc.tile_pool(name="keep", bufs=1))
         work = ctx.enter_context(tc.tile_pool(name="work", bufs=3))
-        zpool = ctx.enter_context(tc.psum_pool(name="zpool", bufs=6))
-        ypool = ctx.enter_context(tc.psum_pool(name="ypool", bufs=2))
+        zpool = ctx.enter_context(tc.psum_pool(name="zpool", bufs=7))
+        ypool = ctx.enter_context(tc.psum_pool(name="ypool", bufs=1))
 
         offsets = keep.tile([P, J // 16], U16, name="offsets")
         tab_s = keep.tile([P, T], U8, name="tab_s", tag="tab_s", align_bytes=64)
@@ -50,8 +50,8 @@ def tile_list_meltab_norm_kernel(
         gain = keep.tile([P, PASSES * PACK], F32, name="gain", tag="gain")
 
         zeros = keep.tile([P, FILL], I32, name="zeros", tag="table", align_bytes=64)
-        nc.gpsimd.memset(tab_s[:].bitcast(I32), 0)
         nc.vector.memset(zeros[:], 0)
+        nc.vector.memset(tab_s[:].bitcast(I32), 0)
         for i in range(2):
             nc.vector.tensor_copy(
                 raw_s[i][:].bitcast(I32).rearrange("p (a c) -> p a c", c=FILL),
@@ -61,9 +61,9 @@ def tile_list_meltab_norm_kernel(
             keep.tile([P, HALF + 2 * F], U8, name="stage0", tag="stage0", align_bytes=64),
             keep.tile([P, HALF + PASSES * N], U8, name="stage1", tag="stage1", align_bytes=64),
         ]
-        nc.gpsimd.memset(early[:].bitcast(I32), 0)
-        nc.gpsimd.memset(late[:].bitcast(I32), 0)
-        nc.gpsimd.memset(stage[1][:, HALF:].bitcast(I32), 0)
+        nc.vector.memset(early[:].bitcast(I32), 0)
+        nc.vector.memset(late[:].bitcast(I32), 0)
+        nc.vector.memset(stage[1][:, HALF:].bitcast(I32), 0)
         tab_w = keep.tile([P, T], U32, name="tab_w", tag="table", align_bytes=64)
 
         nc.sync.dma_start(offsets[:], offs)
@@ -148,6 +148,7 @@ def tile_list_meltab_norm_kernel(
             j0, w, b = units[u]
             g, c0 = divmod(j0, HALF)
             sq = work.tile([P, PACK, 2 * w], F32, name="sq")
+            banks = []
             for t in range(PACK):
                 s = b * PACK + t
                 z = zpool.tile([P, 2 * w], F32, name="z")
@@ -162,7 +163,10 @@ def tile_list_meltab_norm_kernel(
                         start=True,
                         stop=True,
                     )
-                nc.scalar.activation(out=sq[:, t, :], in_=z[:], func=ACT.Square, scale=root[:, s : s + 1])
+                banks.append(z)
+            for t in (3, 0, 1, 2):
+                s = b * PACK + t
+                nc.scalar.activation(out=sq[:, t, :], in_=banks[t][:], func=ACT.Square, scale=root[:, s : s + 1])
             squares[u] = sq
 
         def add(u):
@@ -217,6 +221,8 @@ def tile_list_meltab_norm_kernel(
 
         n = len(units)
         for step in range(n + 3):
+            if 0 <= step - 3 < n:
+                finish(step - 3)
             if step < n:
                 transform(step)
             if 0 <= step - 1 < n:
@@ -225,5 +231,3 @@ def tile_list_meltab_norm_kernel(
                 filters(step - 2)
             if 0 <= step - 1 < n:
                 sign(step - 1)
-            if 0 <= step - 3 < n:
-                finish(step - 3)

from contextlib import ExitStack

import concourse.mybir as mybir

K, F, N, T, J = 512, 1024, 128, 4096, 1024
FLOPS = 2 * (2 * K * F * J + F * N * J)

F32 = mybir.dt.float32
BF16 = mybir.dt.bfloat16
I32 = mybir.dt.int32
U32 = mybir.dt.uint32
U16 = mybir.dt.uint16
U8 = mybir.dt.uint8
FP8X4 = mybir.dt.float8_e4m3fn_x4
FP4X4 = mybir.dt.float4_e2m1fn_x4
ALU = mybir.AluOpType
ACT = mybir.ActivationFunctionType

P = 128
PACK = 4
PASSES = F // (P * PACK)
HALF = 512
WIDTHS = (256, 256, 256, 128, 128)
ROW_STEP = 8
FILL = 64
TINY = 2.0**-112
TAIL = 512


def tile_list_meltab_norm_kernel(
    tc, tab_words, tab_scales, co_words, co_scales, si_words, si_scales, gn, fb_words, fb_scales, mu, isd, offs, out
):
    nc = tc.nc
    with ExitStack() as ctx:
        keep = ctx.enter_context(tc.tile_pool(name="keep", bufs=1))
        work = ctx.enter_context(tc.tile_pool(name="work", bufs=3))
        zpool = ctx.enter_context(tc.psum_pool(name="zpool", bufs=7))
        ypool = ctx.enter_context(tc.psum_pool(name="ypool", bufs=1))

        offsets = keep.tile([P, J // 16], U16, name="offsets")
        tab_s = keep.tile([P, T], U8, name="tab_s", tag="tab_s", align_bytes=64)
        raw_s = [
            keep.tile([P, F], U8, name="raw_s0", align_bytes=64),
            keep.tile([P, F], U8, name="raw_s1", align_bytes=64),
        ]
        early = keep.tile([P, HALF + 2 * F], U8, name="early", align_bytes=64)
        late = keep.tile([P, HALF + PASSES * N], U8, name="late", align_bytes=64)
        raw_w = [keep.tile([P, 2 * F], U8, name="raw_w%d" % i, tag="raw_w%d" % i, align_bytes=64) for i in range(2)]
        wts = [keep.tile([P, 2 * F], U8, name="wts%d" % i, align_bytes=64) for i in range(2)]
        gain = keep.tile([P, PASSES * PACK], F32, name="gain", tag="gain")

        zeros = keep.tile([P, FILL], I32, name="zeros", tag="table", align_bytes=64)
        nc.vector.memset(zeros[:], 0)
        nc.vector.memset(tab_s[:].bitcast(I32), 0)
        for i in range(2):
            nc.vector.tensor_copy(
                raw_s[i][:].bitcast(I32).rearrange("p (a c) -> p a c", c=FILL),
                zeros[:].unsqueeze(1).to_broadcast([P, F // 4 // FILL, FILL]),
            )
        stage = [
            keep.tile([P, HALF + 2 * F], U8, name="stage0", tag="stage0", align_bytes=64),
            keep.tile([P, HALF + PASSES * N], U8, name="stage1", tag="stage1", align_bytes=64),
        ]
        nc.vector.memset(early[:].bitcast(I32), 0)
        nc.vector.memset(late[:].bitcast(I32), 0)
        nc.vector.memset(stage[1][:, HALF:].bitcast(I32), 0)
        tab_w = keep.tile([P, T], U32, name="tab_w", tag="table", align_bytes=64)

        nc.sync.dma_start(offsets[:], offs)
        nc.sync.dma_start(out=raw_w[0][:].bitcast(I32), in_=co_words[0].bitcast(I32))
        nc.sync.dma_start(out=raw_w[1][:].bitcast(I32), in_=si_words[0].bitcast(I32))
        nc.scalar.dma_start(
            out=gain[:].rearrange("p (b t) -> p b t", t=PACK), in_=gn.rearrange("(b p t) -> p b t", p=P, t=PACK)
        )
        nc.sync.dma_start(out=tab_s[0:P:ROW_STEP, :].bitcast(I32), in_=tab_scales[0].bitcast(I32))
        nc.sync.dma_start(out=raw_s[0][0:P:ROW_STEP, :].bitcast(I32), in_=co_scales[0].bitcast(I32))
        nc.sync.dma_start(out=raw_s[1][0:P:ROW_STEP, :].bitcast(I32), in_=si_scales[0].bitcast(I32))
        nc.sync.dma_start(out=tab_w[:].bitcast(I32), in_=tab_words[0].rearrange("p t i -> p (t i)").bitcast(I32))
        nc.sync.dma_start(
            out=stage[1][0:P:ROW_STEP, HALF:].bitcast(I32).rearrange("q (a n) -> q a n", a=PASSES),
            in_=fb_scales.bitcast(I32).rearrange("a q n -> q a n"),
        )

        small = [P, PASSES * PACK]
        mag = keep.tile(small, F32, name="mag")
        sgn = keep.tile(small, BF16, name="sgn")
        guess = keep.tile(small, F32, name="guess")
        inv = keep.tile(small, F32, name="inv")
        quot = keep.tile(small, F32, name="quot")
        root = keep.tile(small, F32, name="root")
        nc.scalar.activation(out=mag[:], in_=gain[:], func=ACT.Abs)
        nc.scalar.activation(out=guess[:], in_=mag[:], func=ACT.Sqrt, bias=TINY)
        nc.scalar.activation(out=sgn[:], in_=gain[:], func=ACT.Sign)

        for i in range(2):
            nc.vector.tensor_copy(
                wts[i][:].bitcast(U16).rearrange("p (b t m) -> p b t m", t=PACK, m=P),
                raw_w[i][:].bitcast(U16).rearrange("p (b m t) -> p b t m", t=PACK, m=P),
            )
        lists = [offsets[:, g * (HALF // 16) : (g + 1) * (HALF // 16)] for g in range(2)]
        planes = (early, late)

        def look_up_scales(g):
            got_s = keep.tile([P, HALF], U8, name="got_s%d" % g, tag=("got0", "stage0")[g], align_bytes=64)
            nc.vector.tensor_copy(got_s[:], tab_s[:].indirect(lists[g]))
            nc.vector.tensor_copy(stage[g][:, 0:HALF].bitcast(I32), got_s[:].bitcast(I32))

        def place_rows(g):
            for r in range(4):
                (nc.scalar if g == 0 and r % 2 == 0 else nc.sync).dma_start(
                    out=planes[g][r:P:32, :].bitcast(I32), in_=stage[g][ROW_STEP * r : P : 32, :].bitcast(I32)
                )

        def look_up_words(g):
            picked = keep.tile([P, HALF], U32, name="got_w%d" % g, tag=("got0", "stage0")[g], align_bytes=64)
            nc.vector.tensor_copy(picked[:], tab_w[:].indirect(lists[g]))
            return picked

        look_up_scales(0)
        for i in range(2):
            nc.vector.tensor_copy(
                stage[0][:, HALF + F * i : HALF + F * (i + 1)].rearrange("p (b t m) -> p b t m", t=PACK, m=P),
                raw_s[i][:].rearrange("p (b m t) -> p b t m", t=PACK, m=P),
            )
        place_rows(0)
        fb_w = keep.tile([P, PASSES, N], U32, name="fb_w", tag="raw_w0", align_bytes=64)
        nc.sync.dma_start(out=fb_w[:].bitcast(I32), in_=fb_words.rearrange("a p n i -> p a (n i)").bitcast(I32))
        nc.vector.reciprocal(inv[:], guess[:])
        nc.vector.scalar_tensor_tensor(quot[:], mag[:], 0.5, inv[:], ALU.mult, ALU.mult)
        nc.vector.scalar_tensor_tensor(root[:], guess[:], 0.5, quot[:], ALU.mult, ALU.add)
        got_w = [look_up_words(0)]
        look_up_scales(1)
        place_rows(1)
        got_w.append(look_up_words(1))

        mu_c = keep.tile([P, 1], F32, name="mu_c", tag="gain")
        isd_c = keep.tile([P, 1], F32, name="isd_c", tag="tab_s", align_bytes=64)
        shift = keep.tile([P, 1], F32, name="shift")
        with nc.allow_non_contiguous_dma(reason="one value a partition"):
            nc.sync.dma_start(out=mu_c[:], in_=mu.rearrange("(p o) -> p o", o=1))
            nc.sync.dma_start(out=isd_c[:], in_=isd.rearrange("(p o) -> p o", o=1))
        nc.gpsimd.tensor_scalar(shift[:], mu_c[:], isd_c[:], -1.0, ALU.mult, ALU.mult)

        units = [(sum(WIDTHS[:c]), w, b) for c, w in enumerate(WIDTHS) for b in range(PASSES)]
        squares, power, signed, acc = {}, {}, {}, {}

        def transform(u):
            j0, w, b = units[u]
            g, c0 = divmod(j0, HALF)
            sq = work.tile([P, PACK, 2 * w], F32, name="sq")
            banks = []
            for t in range(PACK):
                s = b * PACK + t
                z = zpool.tile([P, 2 * w], F32, name="z")
                for i in range(2):
                    base = HALF + F * i + P * s
                    nc.tensor.matmul_mx(
                        out=z[:, i * w : (i + 1) * w],
                        lhsT=wts[i][:, 2 * P * s : 2 * P * (s + 1)].bitcast(FP4X4),
                        lhsT_scale=early[:, base : base + P],
                        rhs=got_w[g][:, c0 : c0 + w].bitcast(FP8X4),
                        rhs_scale=planes[g][:, c0 : c0 + w],
                        start=True,
                        stop=True,
                    )
                banks.append(z)
            for t in (3, 0, 1, 2):
                s = b * PACK + t
                nc.scalar.activation(out=sq[:, t, :], in_=banks[t][:], func=ACT.Square, scale=root[:, s : s + 1])
            squares[u] = sq

        def add(u):
            w = units[u][1]
            sq = squares[u]
            h = work.tile([P, w * PACK], BF16, name="h", align_bytes=64)
            nc.vector.tensor_tensor(
                h[:].rearrange("p (c i t) -> p c t i", i=2, t=PACK),
                sq[:, :, 0:w].rearrange("p t (c i) -> p c t i", i=2),
                sq[:, :, w:].rearrange("p t (c i) -> p c t i", i=2),
                ALU.add,
            )
            power[u] = h

        def sign(u):
            j0, w, b = units[u]
            hs = work.tile([P, w * PACK], BF16, name="hs", align_bytes=64)
            nc.vector.tensor_tensor(
                hs[:].rearrange("p (c t) -> p c t", t=PACK),
                power[u][:].rearrange("p (c t) -> p c t", t=PACK),
                sgn[:, b * PACK : (b + 1) * PACK].unsqueeze(1).to_broadcast([P, w, PACK]),
                ALU.mult,
            )
            signed[u] = hs

        def filters(u):
            j0, w, b = units[u]
            codes = work.tile([P, w], U32, name="codes", align_bytes=64)
            scales = work.tile([P, w], U8, name="scales", align_bytes=64)
            nc.vector.quantize_mx(out=codes[:].bitcast(FP8X4), scales=scales[:], in_=signed[u][:])
            if b == 0:
                acc[j0] = ypool.tile([P, w], F32, name="y")
            nc.tensor.matmul_mx(
                out=acc[j0][:],
                lhsT=fb_w[:, b, :].bitcast(FP8X4),
                lhsT_scale=late[:, HALF + N * b : HALF + N * (b + 1)],
                rhs=codes[:].bitcast(FP8X4),
                rhs_scale=scales[:],
                start=(b == 0),
                stop=(b == PASSES - 1),
            )

        def finish(u):
            j0, w, b = units[u]
            if b == PASSES - 1:
                res = work.tile([P, w], F32, name="res")
                if j0 + w > J - TAIL:
                    nc.scalar.activation(out=res[:], in_=acc[j0][:], func=ACT.Identity, scale=isd_c[:], bias=shift[:])
                else:
                    nc.vector.tensor_scalar(res[:], acc[j0][:], isd_c[:], shift[:], ALU.mult, ALU.add)
                nc.sync.dma_start(out=out[:, j0 : j0 + w], in_=res[:])

        n = len(units)
        for step in range(n + 3):
            if 0 <= step - 3 < n:
                finish(step - 3)
            if step < n:
                transform(step)
            if 0 <= step - 1 < n:
                add(step - 1)
            if 0 <= step - 2 < n:
                filters(step - 2)
            if 0 <= step - 1 < n:
                sign(step - 1)
